import numpy as np
import ml_dtypes


def mxq(x, axis, fmt="e4m3"):
    dtype, down = {"e4m3": (ml_dtypes.float8_e4m3fn, 7), "e5m2": (ml_dtypes.float8_e5m2, 14)}[fmt]
    v = np.moveaxis(np.asarray(x, np.float32).astype(ml_dtypes.bfloat16).astype(np.float64), axis, -1)
    blocks = v.reshape(v.shape[:-1] + (-1, 32))
    amax = np.abs(blocks).max(-1, keepdims=True)
    byte = np.maximum(np.where(amax > 0, np.frexp(amax)[1] - 1 + 127, 0) - down, 1)
    scale = np.exp2(byte - 127.0)
    codes = (blocks / scale).astype(np.float32).astype(dtype).astype(np.float64)
    return np.moveaxis((codes * scale).reshape(v.shape), -1, axis)


WIDE = False


def mx_kscale(k):
    if not WIDE:
        return np.ones(k)
    levels = np.array([30, -30])
    if k % 512:
        return np.exp2(np.random.permutation(np.resize(levels, k // 32))).repeat(32)
    a = np.empty((k // 512, 16))
    for p in range(k // 512):
        a[p, :8] = np.random.permutation(np.resize(levels, 8))
        for g in range(8):
            far = levels[np.abs(levels - a[p, g]) >= 10]
            a[p, g + 8] = far[np.random.randint(len(far))]
    return np.exp2(a.ravel()).repeat(32)


def f64(x):
    return np.asarray(x).astype(np.float64)


def striped(idx):
    return np.tile(np.asarray(idx).reshape(-1, 16).T, (8, 1)).astype(np.uint16)


def unstriped(offs):
    return offs[:16].T.reshape(-1).astype(np.int64)


E2M1 = np.array([0.0, 0.5, 1.0, 1.5, 2.0, 3.0, 4.0, 6.0, -0.0, -0.5, -1.0, -1.5, -2.0, -3.0, -4.0, -6.0])


def pack_weight(w, fmt):
    k, n = w.shape
    w = f64(np.asarray(w, np.float32).astype(ml_dtypes.bfloat16)).reshape(k // 32, 32, n)
    amax = np.abs(w).max(1)
    if fmt in ("e4m3", "e5m2"):
        byte = np.frexp(amax)[1] - 1 + 127 - (7 if fmt == "e4m3" else 14)
    else:
        mant, ex = np.frexp(amax / 6.0)
        byte = np.where(mant > 0.5, ex, ex - 1) + 127
    byte = np.clip(np.where(amax > 0, byte, 1), 1, 254)
    scaled = (w * np.exp2(127.0 - byte)[:, None, :]).reshape(k, n).astype(np.float32)
    by_word = np.ascontiguousarray(scaled.reshape(k // 512, 128, 4, n).transpose(0, 1, 3, 2))
    if fmt in ("e4m3", "e5m2"):
        words = by_word.astype(ml_dtypes.float8_e4m3fn if fmt == "e4m3" else ml_dtypes.float8_e5m2).view(np.uint8)
    else:
        c = by_word.astype(ml_dtypes.float4_e2m1fn).view(np.uint8) & 0xF
        words = (c[..., 0::2] | (c[..., 1::2] << 4)).reshape(k // 512, 128, 2 * n)
    return np.ascontiguousarray(words), np.ascontiguousarray(byte.astype(np.uint8).reshape(k // 512, 16, n))


def unpack_weight(words, scales, fmt):
    g, _, n = scales.shape
    words = np.ascontiguousarray(words).reshape(g, 128, n, -1)
    if fmt in ("e4m3", "e5m2"):
        vals = words.view(ml_dtypes.float8_e4m3fn if fmt == "e4m3" else ml_dtypes.float8_e5m2).astype(np.float64)
    else:
        nib = np.empty((g, 128, n, 4), np.uint8)
        nib[..., 0::2] = words & 0xF
        nib[..., 1::2] = words >> 4
        vals = E2M1[nib]
    vals = vals * np.repeat(np.exp2(scales.astype(np.float64) - 127.0), 8, axis=1)[..., None]
    return vals.transpose(0, 1, 3, 2).reshape(g * 512, n)


def sigmoid(v):
    return 1.0 / (1.0 + np.exp(-v))


def sgn(shape):
    return np.random.uniform(0.5, 2.0, shape) * np.where(np.random.standard_normal(shape) < 0, -1.0, 1.0)


K, T, J, R, F, Z, O, N, E = 512, 1024, 256, 512, 512, 1024, 128, 256, 1024


def setup_inputs():
    n = np.random.standard_normal
    idx = np.random.permutation(T)[:J]
    idx2 = np.random.permutation(Z)[:J]
    idx3 = np.random.permutation(J)[:O]
    idx4 = np.random.permutation(J)[:O]
    idx5 = np.random.permutation(J)[:O]
    idx6 = np.random.permutation(E)[:O]
    fk = mx_kscale(K)
    ff = mx_kscale(F)
    fr = mx_kscale(R)
    xtp = pack_weight(n((K, T)) / fk[:, None], "e5m2")
    xop = pack_weight(n((F, Z)) / ff[:, None], "e4m3")
    wp = pack_weight(n((K, R)) * 1 / np.sqrt(K) * fk[:, None], "e2m1")
    w0p = pack_weight(n((F, R)) * 1 / np.sqrt(F) * ff[:, None], "e2m1")
    wbp = pack_weight(n((R, N)) * 1 / np.sqrt(R) / fr[:, None], "e2m1")
    return {
        "xt_words": xtp[0],
        "xt_scales": xtp[1],
        "xo_words": xop[0],
        "xo_scales": xop[1],
        "w_words": wp[0],
        "w_scales": wp[1],
        "w0_words": w0p[0],
        "w0_scales": w0p[1],
        "sa": (np.random.uniform(0.5, 1.6, (R, 1)) * fr[:, None]).astype(np.float32),
        "sb": (np.random.uniform(0.5, 1.6, (R, 1)) * fr[:, None]).astype(np.float32),
        "sg": (sgn((R, 1))).astype(np.float32),
        "bg": (np.random.uniform(-2.0, 2.0, (R, 1))).astype(np.float32),
        "wb_words": wbp[0],
        "wb_scales": wbp[1],
        "offs": striped(idx),
        "offs2": striped(idx2),
        "offs3": striped(idx3),
        "offs4": striped(idx4),
        "offs5": striped(idx5),
        "offs6": striped(idx6),
    }


def reference(xt_words, xt_scales, xo_words, xo_scales, w_words, w_scales, w0_words, w0_scales, sa, sb, sg, bg, wb_words, wb_scales, offs, offs2, offs3, offs4, offs5, offs6):
    idx = unstriped(offs)
    idx2 = unstriped(offs2)
    idx3 = unstriped(offs3)
    idx4 = unstriped(offs4)
    idx5 = unstriped(offs5)
    idx6 = unstriped(offs6)
    xtu = unpack_weight(xt_words, xt_scales, "e5m2")
    xou = unpack_weight(xo_words, xo_scales, "e4m3")
    wu = unpack_weight(w_words, w_scales, "e2m1")
    w0u = unpack_weight(w0_words, w0_scales, "e2m1")
    wbu = unpack_weight(wb_words, wb_scales, "e2m1")
    xtidxg = xtu[:, idx]
    xoidx2g = xou[:, idx2]
    a = wu.T @ xtidxg + w0u.T @ xoidx2g
    hid = np.abs(a[:, idx3] * f64(sa) - a[:, idx4] * f64(sb)) * sigmoid(a[:, idx5] * f64(sg) + f64(bg))
    hidq = mxq(hid, 0, "e4m3")
    p = wbu.T @ hidq
    y = np.zeros((N, E))
    y[:, idx6] = p
    return y

@@ -1,0 +1,176 @@
+from contextlib import ExitStack
+
+import concourse.mybir as mybir
+
+K, T, J, R, O, N, E = 512, 1024, 256, 512, 128, 256, 1024
+P = 128
+PACK = 4
+FLOPS = 2 * K * R * J * 2 + 2 * R * N * O
+
+F32 = mybir.dt.float32
+BF16 = mybir.dt.bfloat16
+I32 = mybir.dt.int32
+U32 = mybir.dt.uint32
+U16 = mybir.dt.uint16
+U8 = mybir.dt.uint8
+E4M3 = mybir.dt.float8_e4m3fn_x4
+E5M2 = mybir.dt.float8_e5m2_x4
+E2M1 = mybir.dt.float4_e2m1fn_x4
+ACT = mybir.ActivationFunctionType
+ALU = mybir.AluOpType
+
+
+def tile_list_gatedlarger_bank_one_scattered_kernel(
+    tc, xt_words, xt_scales, xo_words, xo_scales, w_words, w_scales, w0_words, w0_scales,
+    sa, sb, sg, bg, wb_words, wb_scales, offs, offs2, offs3, offs4, offs5, offs6, out,
+):
+    nc = tc.nc
+    with ExitStack() as ctx:
+        pool = ctx.enter_context(tc.tile_pool(name="held", bufs=1))
+        psum = ctx.enter_context(tc.psum_pool(name="psum", bufs=1))
+
+        def load_list(src, name):
+            lst = pool.tile(list(src.shape), U16, name=name)
+            nc.sync.dma_start(lst[:], src)
+            return lst
+
+        def load_half_rows(dst, scales):
+            rows = scales[0].bitcast(I32).rearrange("(h g r) n -> g r h n", h=2, g=2)
+            for g in range(2):
+                nc.scalar.dma_start(dst[32 * g : 32 * g + 4].bitcast(I32), rows[g])
+
+        xt_stage = pool.tile([64, 2, T], U8, name="xt_stage")
+        xo_stage = pool.tile([64, 2, T], U8, name="xo_stage")
+        ws_raw = pool.tile([P, 2, 2 * R], U8, name="ws_raw")
+        wb_plane = pool.tile([P, N], U8, name="wb_plane", align_bytes=64)
+        nc.vector.memset(xt_stage[:].bitcast(I32), 0)
+        nc.gpsimd.memset(xo_stage[:].bitcast(I32), 0)
+        nc.vector.memset(ws_raw[0:64].bitcast(I32), 0)
+        nc.gpsimd.memset(wb_plane[:].bitcast(I32), 0)
+
+        w_raw = pool.tile([P, 2 * R], U8, name="w_raw")
+        w0_raw = pool.tile([P, 2 * R], U8, name="w0_raw")
+        xt_table = pool.tile([P, T], U32, name="xt_table")
+        xo_table = pool.tile([P, T], U32, name="xo_table")
+        idx = load_list(offs, "idx")
+        nc.sync.dma_start(w_raw[:].bitcast(I32), w_words[0].bitcast(I32))
+        nc.sync.dma_start(w0_raw[:].bitcast(I32), w0_words[0].bitcast(I32))
+        load_half_rows(xt_stage, xt_scales)
+        nc.sync.dma_start(xt_table[:].bitcast(I32), xt_words[0].rearrange("p n t -> p (n t)").bitcast(I32))
+        nc.sync.dma_start(xo_table[:].bitcast(I32), xo_words[0].rearrange("p n t -> p (n t)").bitcast(I32))
+        idx2 = load_list(offs2, "idx2")
+        load_half_rows(xo_stage, xo_scales)
+        load_half_rows(ws_raw[:, :, 0:R], w_scales)
+        load_half_rows(ws_raw[:, :, R : 2 * R], w0_scales)
+        idx5 = load_list(offs5, "idx5")
+        idx3 = load_list(offs3, "idx3")
+        idx4 = load_list(offs4, "idx4")
+        cols = {}
+        for name, src in (("sg", sg), ("bg", bg), ("sa", sa), ("sb", sb)):
+            cols[name] = pool.tile([P, PACK], F32, name=name + "_cols")
+            nc.sync.dma_start(cols[name][:], src.rearrange("(p t) one -> p (t one)", t=PACK))
+        idx6 = load_list(offs6, "idx6")
+        wb_codes = pool.tile([P, 2 * N], U8, name="wb_codes", align_bytes=64)
+        nc.gpsimd.dma_start(wb_codes[:].bitcast(I32), wb_words[0].bitcast(I32))
+        for q in range(4):
+            nc.gpsimd.dma_start(wb_plane[32 * q : 32 * q + 4, :].bitcast(I32), wb_scales[0, 4 * q : 4 * q + 4, :].bitcast(I32))
+
+        pages = [pool.tile([P, E], F32, name=f"page{h}") for h in range(2)]
+        for page in pages:
+            nc.vector.memset(page[:], 0.0)
+
+        w_codes = pool.tile([P, 2 * R], U8, name="w_codes", align_bytes=64)
+        w0_codes = pool.tile([P, 2 * R], U8, name="w0_codes", align_bytes=64)
+        for dst, src in ((w_codes, w_raw), (w0_codes, w0_raw)):
+            nc.scalar.copy(
+                dst[:].bitcast(U16).rearrange("p (t m) -> p t m", t=PACK),
+                src[:].bitcast(U16).rearrange("p (m t) -> p t m", t=PACK),
+            )
+
+        def gather_table(stage, table, lst, name):
+            plane = pool.tile([P, T], U8, name=name + "_plane")
+            for h in range(2):
+                nc.vector.tensor_copy(plane[64 * h : 64 * h + 64, :].bitcast(I32), stage[:, h, :].bitcast(I32))
+            picked_scales = pool.tile([P, J], U8, name=name + "_scales", align_bytes=64)
+            nc.vector.tensor_copy(picked_scales[:], plane[:].indirect(lst[:]))
+            picked_words = pool.tile([P, J], U32, name=name + "_words", align_bytes=64)
+            nc.vector.tensor_copy(picked_words[:], table[:].indirect(lst[:]))
+            return picked_words, picked_scales
+
+        xt_w, xt_s = gather_table(xt_stage, xt_table, idx, "xt")
+        xo_w, xo_s = gather_table(xo_stage, xo_table, idx2, "xo")
+
+        nc.vector.tensor_copy(ws_raw[64:128, 0, :].bitcast(I32), ws_raw[0:64, 1, :].bitcast(I32))
+        w_planes = pool.tile([P, PACK, 2, P], U8, name="w_planes", align_bytes=64)
+        dealt = ws_raw[:, 0, :].rearrange("p (i m t) -> p t i m", i=2, t=PACK)
+        hidden = []
+        for t in range(PACK):
+            nc.vector.tensor_copy(w_planes[:, t], dealt[:, t])
+        for t in range(PACK):
+            acc = psum.tile([P, J], F32, name=f"acc{t}")
+            codes = slice(2 * P * t, 2 * P * (t + 1))
+            nc.tensor.matmul_mx(acc[:], lhsT=w_codes[:, codes].bitcast(E2M1), lhsT_scale=w_planes[:, t, 0],
+                                rhs=xt_w[:].bitcast(E5M2), rhs_scale=xt_s[:], start=True, stop=False)
+            nc.tensor.matmul_mx(acc[:], lhsT=w0_codes[:, codes].bitcast(E2M1), lhsT_scale=w_planes[:, t, 1],
+                                rhs=xo_w[:].bitcast(E4M3), rhs_scale=xo_s[:], start=False, stop=True)
+            rows = pool.tile([P, J], F32, name=f"hidden{t}")
+            nc.vector.tensor_copy(rows[:], acc[:])
+            hidden.append(rows)
+
+        first = pool.tile([P, PACK, O], F32, name="first")
+        second = pool.tile([P, PACK, O], F32, name="second")
+        gate = pool.tile([P, PACK, O], F32, name="gate")
+        diff = pool.tile([P, PACK, O], F32, name="diff")
+        size = pool.tile([P, PACK, O], F32, name="size")
+        hid = pool.tile([P, O, PACK], BF16, name="hid", align_bytes=64)
+
+        def fetch_gate(t):
+            nc.scalar.activation(gate[:, t], hidden[t][:].indirect(idx5[:]), ACT.Sigmoid,
+                                 bias=cols["bg"][:, t : t + 1], scale=cols["sg"][:, t : t + 1])
+
+        def fetch_pair(t):
+            nc.scalar.activation(first[:, t], hidden[t][:].indirect(idx3[:]), ACT.Copy, scale=cols["sa"][:, t : t + 1])
+            nc.scalar.activation(second[:, t], hidden[t][:].indirect(idx4[:]), ACT.Copy, scale=cols["sb"][:, t : t + 1])
+
+        def subtract(ts):
+            nc.vector.tensor_tensor(diff[:, ts], first[:, ts], second[:, ts], ALU.subtract)
+
+        def magnitude(ts):
+            nc.vector.scalar_tensor_tensor(size[:, ts], diff[:, ts], -1.0, diff[:, ts], ALU.mult, ALU.max)
+
+        def gated(ts):
+            nc.vector.tensor_tensor(hid[:, :, ts], size[:, ts].rearrange("p t o -> p o t"),
+                                    gate[:, ts].rearrange("p t o -> p o t"), ALU.mult)
+
+        fetch_gate(0)
+        for t in range(PACK):
+            fetch_pair(t)
+        for t in range(1, PACK):
+            fetch_gate(t)
+        subtract(slice(0, 2))
+        magnitude(slice(0, 2))
+        subtract(slice(2, 3))
+        gated(slice(0, 1))
+        magnitude(slice(2, 3))
+        subtract(slice(3, 4))
+        magnitude(slice(3, 4))
+        gated(slice(1, 4))
+
+        hid_words = pool.tile([P, O], U32, name="hid_words", align_bytes=64)
+        hid_scales = pool.tile([P, O], U8, name="hid_scales", align_bytes=64)
+        nc.vector.quantize_mx(hid_words[:].bitcast(E4M3), hid_scales[:], hid[:].rearrange("p o t -> p (o t)"))
+
+        for h in range(2):
+            acc = psum.tile([P, O], F32, name=f"result{h}")
+            nc.tensor.matmul_mx(acc[:], lhsT=wb_codes[:, 2 * P * h : 2 * P * (h + 1)].bitcast(E2M1),
+                                lhsT_scale=wb_plane[:, P * h : P * (h + 1)],
+                                rhs=hid_words[:].bitcast(E4M3), rhs_scale=hid_scales[:], start=True, stop=True)
+            values = pool.tile([P, O], F32, name=f"values{h}")
+            if h == 0:
+                nc.vector.tensor_copy(values[:], acc[:])
+                nc.vector.tensor_copy(pages[h][:].indirect(idx6[:]), values[:])
+                nc.sync.dma_start(out[P * h : P * (h + 1), :], pages[h][:])
+            else:
+                nc.scalar.copy(values[:], acc[:])
+                nc.scalar.activation(pages[h][:].indirect(idx6[:]), values[:], ACT.Copy)
+                nc.scalar.dma_start(out[P * h : P * (h + 1), :], pages[h][:])

@@ -34,10 +34,12 @@ def tile_list_gatedlarger_bank_one_scattered_kernel(
             nc.sync.dma_start(lst[:], src)
             return lst
 
-        def load_half_rows(dst, scales):
-            rows = scales[0].bitcast(I32).rearrange("(h g r) n -> g r h n", h=2, g=2)
+        def half_rows(scales):
+            return scales[0].bitcast(I32).rearrange("(h g r) n -> g r h n", h=2, g=2)
+
+        def load_half_rows(queue, dst, scales):
             for g in range(2):
-                nc.scalar.dma_start(dst[32 * g : 32 * g + 4].bitcast(I32), rows[g])
+                queue.dma_start(dst[32 * g : 32 * g + 4].bitcast(I32), half_rows(scales)[g])
 
         xt_stage = pool.tile([64, 2, T], U8, name="xt_stage")
         xo_stage = pool.tile([64, 2, T], U8, name="xo_stage")
@@ -46,73 +48,75 @@ def tile_list_gatedlarger_bank_one_scattered_kernel(
         nc.vector.memset(xt_stage[:].bitcast(I32), 0)
         nc.gpsimd.memset(xo_stage[:].bitcast(I32), 0)
         nc.vector.memset(ws_raw[0:64].bitcast(I32), 0)
-        nc.gpsimd.memset(wb_plane[:].bitcast(I32), 0)
+        nc.vector.memset(wb_plane[:].bitcast(I32), 0)
 
-        w_raw = pool.tile([P, 2 * R], U8, name="w_raw")
-        w0_raw = pool.tile([P, 2 * R], U8, name="w0_raw")
+        w_raw = pool.tile([P, 2, R], U16, name="w_raw")
         xt_table = pool.tile([P, T], U32, name="xt_table")
         xo_table = pool.tile([P, T], U32, name="xo_table")
         idx = load_list(offs, "idx")
-        nc.sync.dma_start(w_raw[:].bitcast(I32), w_words[0].bitcast(I32))
-        nc.sync.dma_start(w0_raw[:].bitcast(I32), w0_words[0].bitcast(I32))
-        load_half_rows(xt_stage, xt_scales)
+        idx2 = load_list(offs2, "idx2")
+        nc.sync.dma_start(w_raw[:, 0].bitcast(I32), w_words[0].bitcast(I32))
+        nc.sync.dma_start(w_raw[:, 1].bitcast(I32), w0_words[0].bitcast(I32))
+        load_half_rows(nc.sync, xt_stage, xt_scales)
+        load_half_rows(nc.sync, xo_stage, xo_scales)
         nc.sync.dma_start(xt_table[:].bitcast(I32), xt_words[0].rearrange("p n t -> p (n t)").bitcast(I32))
         nc.sync.dma_start(xo_table[:].bitcast(I32), xo_words[0].rearrange("p n t -> p (n t)").bitcast(I32))
-        idx2 = load_list(offs2, "idx2")
-        load_half_rows(xo_stage, xo_scales)
-        load_half_rows(ws_raw[:, :, 0:R], w_scales)
-        load_half_rows(ws_raw[:, :, R : 2 * R], w0_scales)
+        load_half_rows(nc.sync, ws_raw[:, :, 0:R], w_scales)
+        load_half_rows(nc.sync, ws_raw[:, :, R : 2 * R], w0_scales)
         idx5 = load_list(offs5, "idx5")
         idx3 = load_list(offs3, "idx3")
         idx4 = load_list(offs4, "idx4")
         cols = {}
         for name, src in (("sg", sg), ("bg", bg), ("sa", sa), ("sb", sb)):
             cols[name] = pool.tile([P, PACK], F32, name=name + "_cols")
-            nc.sync.dma_start(cols[name][:], src.rearrange("(p t) one -> p (t one)", t=PACK))
+            nc.gpsimd.dma_start(cols[name][:], src.rearrange("(p t) one -> p (t one)", t=PACK))
         idx6 = load_list(offs6, "idx6")
         wb_codes = pool.tile([P, 2 * N], U8, name="wb_codes", align_bytes=64)
-        nc.gpsimd.dma_start(wb_codes[:].bitcast(I32), wb_words[0].bitcast(I32))
+        nc.sync.dma_start(wb_codes[:].bitcast(I32), wb_words[0].bitcast(I32))
         for q in range(4):
-            nc.gpsimd.dma_start(wb_plane[32 * q : 32 * q + 4, :].bitcast(I32), wb_scales[0, 4 * q : 4 * q + 4, :].bitcast(I32))
+            nc.sync.dma_start(wb_plane[32 * q : 32 * q + 4, :].bitcast(I32), wb_scales[0, 4 * q : 4 * q + 4, :].bitcast(I32))
 
         pages = [pool.tile([P, E], F32, name=f"page{h}") for h in range(2)]
         for page in pages:
             nc.vector.memset(page[:], 0.0)
 
-        w_codes = pool.tile([P, 2 * R], U8, name="w_codes", align_bytes=64)
-        w0_codes = pool.tile([P, 2 * R], U8, name="w0_codes", align_bytes=64)
-        for dst, src in ((w_codes, w_raw), (w0_codes, w0_raw)):
-            nc.scalar.copy(
-                dst[:].bitcast(U16).rearrange("p (t m) -> p t m", t=PACK),
-                src[:].bitcast(U16).rearrange("p (m t) -> p t m", t=PACK),
-            )
-
-        def gather_table(stage, table, lst, name):
+        def gather_scales(stage, lst, name):
             plane = pool.tile([P, T], U8, name=name + "_plane")
             for h in range(2):
                 nc.vector.tensor_copy(plane[64 * h : 64 * h + 64, :].bitcast(I32), stage[:, h, :].bitcast(I32))
-            picked_scales = pool.tile([P, J], U8, name=name + "_scales", align_bytes=64)
-            nc.vector.tensor_copy(picked_scales[:], plane[:].indirect(lst[:]))
-            picked_words = pool.tile([P, J], U32, name=name + "_words", align_bytes=64)
-            nc.vector.tensor_copy(picked_words[:], table[:].indirect(lst[:]))
-            return picked_words, picked_scales
+            picked = pool.tile([P, J], U8, name=name + "_scales", align_bytes=64)
+            nc.vector.tensor_copy(picked[:], plane[:].indirect(lst[:]))
+            return picked
 
-        xt_w, xt_s = gather_table(xt_stage, xt_table, idx, "xt")
-        xo_w, xo_s = gather_table(xo_stage, xo_table, idx2, "xo")
+        def gather_words(table, lst, name):
+            picked = pool.tile([P, J], U32, name=name + "_words", align_bytes=64)
+            nc.vector.tensor_copy(picked[:], table[:].indirect(lst[:]))
+            return picked
 
-        nc.vector.tensor_copy(ws_raw[64:128, 0, :].bitcast(I32), ws_raw[0:64, 1, :].bitcast(I32))
+        w_codes = pool.tile([P, PACK, 2, P], U16, name="w_codes", align_bytes=64)
         w_planes = pool.tile([P, PACK, 2, P], U8, name="w_planes", align_bytes=64)
-        dealt = ws_raw[:, 0, :].rearrange("p (i m t) -> p t i m", i=2, t=PACK)
+        dealt_words = w_raw[:].rearrange("p i (m t) -> p t i m", t=PACK)
+        dealt_scales = ws_raw[:, 0, :].rearrange("p (i m t) -> p t i m", i=2, t=PACK)
+
+        def deal(t):
+            nc.vector.tensor_copy(w_codes[:, t], dealt_words[:, t])
+            nc.vector.tensor_copy(w_planes[:, t], dealt_scales[:, t])
+
+        xt_s = gather_scales(xt_stage, idx, "xt")
+        xo_s = gather_scales(xo_stage, idx2, "xo")
+        xt_w = gather_words(xt_table, idx, "xt")
+        nc.vector.tensor_copy(ws_raw[64:128, 0, :].bitcast(I32), ws_raw[0:64, 1, :].bitcast(I32))
+        deal(0)
+        xo_w = gather_words(xo_table, idx2, "xo")
         hidden = []
         for t in range(PACK):
-            nc.vector.tensor_copy(w_planes[:, t], dealt[:, t])
-        for t in range(PACK):
             acc = psum.tile([P, J], F32, name=f"acc{t}")
-            codes = slice(2 * P * t, 2 * P * (t + 1))
-            nc.tensor.matmul_mx(acc[:], lhsT=w_codes[:, codes].bitcast(E2M1), lhsT_scale=w_planes[:, t, 0],
+            nc.tensor.matmul_mx(acc[:], lhsT=w_codes[:, t, 0].bitcast(E2M1), lhsT_scale=w_planes[:, t, 0],
                                 rhs=xt_w[:].bitcast(E5M2), rhs_scale=xt_s[:], start=True, stop=False)
-            nc.tensor.matmul_mx(acc[:], lhsT=w0_codes[:, codes].bitcast(E2M1), lhsT_scale=w_planes[:, t, 1],
+            nc.tensor.matmul_mx(acc[:], lhsT=w_codes[:, t, 1].bitcast(E2M1), lhsT_scale=w_planes[:, t, 1],
                                 rhs=xo_w[:].bitcast(E4M3), rhs_scale=xo_s[:], start=False, stop=True)
+            if t + 1 < PACK:
+                deal(t + 1)
             rows = pool.tile([P, J], F32, name=f"hidden{t}")
             nc.vector.tensor_copy(rows[:], acc[:])
             hidden.append(rows)

@@ -43,32 +43,32 @@ def tile_list_gatedlarger_bank_one_scattered_kernel(
 
         xt_stage = pool.tile([64, 2, T], U8, name="xt_stage")
         xo_stage = pool.tile([64, 2, T], U8, name="xo_stage")
-        ws_raw = pool.tile([P, 2, 2 * R], U8, name="ws_raw")
+        ws_raw = pool.tile([P, 2, 2 * R], U8, name="ws_raw", tag="scales_then_page")
         wb_plane = pool.tile([P, N], U8, name="wb_plane", align_bytes=64)
-        nc.vector.memset(xt_stage[:].bitcast(I32), 0)
-        nc.gpsimd.memset(xo_stage[:].bitcast(I32), 0)
-        nc.vector.memset(ws_raw[0:64].bitcast(I32), 0)
+        for stage in (xt_stage, xo_stage, ws_raw):
+            nc.vector.memset(stage[0:64, 0].bitcast(I32), 0)
+            nc.gpsimd.memset(stage[0:64, 1].bitcast(I32), 0)
         nc.vector.memset(wb_plane[:].bitcast(I32), 0)
 
         w_raw = pool.tile([P, 2, R], U16, name="w_raw")
         xt_table = pool.tile([P, T], U32, name="xt_table")
-        xo_table = pool.tile([P, T], U32, name="xo_table")
+        xo_table = pool.tile([P, T], U32, name="xo_table", tag="table_planes_page", align_bytes=64)
         idx = load_list(offs, "idx")
         idx2 = load_list(offs2, "idx2")
         nc.sync.dma_start(w_raw[:, 0].bitcast(I32), w_words[0].bitcast(I32))
-        nc.sync.dma_start(w_raw[:, 1].bitcast(I32), w0_words[0].bitcast(I32))
         load_half_rows(nc.sync, xt_stage, xt_scales)
         load_half_rows(nc.sync, xo_stage, xo_scales)
         nc.sync.dma_start(xt_table[:].bitcast(I32), xt_words[0].rearrange("p n t -> p (n t)").bitcast(I32))
-        nc.sync.dma_start(xo_table[:].bitcast(I32), xo_words[0].rearrange("p n t -> p (n t)").bitcast(I32))
         load_half_rows(nc.sync, ws_raw[:, :, 0:R], w_scales)
         load_half_rows(nc.sync, ws_raw[:, :, R : 2 * R], w0_scales)
+        nc.sync.dma_start(w_raw[:, 1].bitcast(I32), w0_words[0].bitcast(I32))
+        nc.sync.dma_start(xo_table[:].bitcast(I32), xo_words[0].rearrange("p n t -> p (n t)").bitcast(I32))
         idx5 = load_list(offs5, "idx5")
         idx3 = load_list(offs3, "idx3")
         idx4 = load_list(offs4, "idx4")
         cols = {}
         for name, src in (("sg", sg), ("bg", bg), ("sa", sa), ("sb", sb)):
-            cols[name] = pool.tile([P, PACK], F32, name=name + "_cols")
+            cols[name] = pool.tile([P, PACK], F32, name=name + "_cols", tag=name + "_cols")
             nc.gpsimd.dma_start(cols[name][:], src.rearrange("(p t) one -> p (t one)", t=PACK))
         idx6 = load_list(offs6, "idx6")
         wb_codes = pool.tile([P, 2 * N], U8, name="wb_codes", align_bytes=64)
@@ -76,60 +76,62 @@ def tile_list_gatedlarger_bank_one_scattered_kernel(
         for q in range(4):
             nc.sync.dma_start(wb_plane[32 * q : 32 * q + 4, :].bitcast(I32), wb_scales[0, 4 * q : 4 * q + 4, :].bitcast(I32))
 
-        pages = [pool.tile([P, E], F32, name=f"page{h}") for h in range(2)]
-        for page in pages:
-            nc.vector.memset(page[:], 0.0)
-
-        def gather_scales(stage, lst, name):
+        def spread_scales(stage, name):
             plane = pool.tile([P, T], U8, name=name + "_plane")
             for h in range(2):
                 nc.vector.tensor_copy(plane[64 * h : 64 * h + 64, :].bitcast(I32), stage[:, h, :].bitcast(I32))
-            picked = pool.tile([P, J], U8, name=name + "_scales", align_bytes=64)
-            nc.vector.tensor_copy(picked[:], plane[:].indirect(lst[:]))
+            return plane
+
+        def gather(window, lst, dtype, name):
+            picked = pool.tile([P, J], dtype, name=name, align_bytes=64)
+            nc.vector.tensor_copy(picked[:], window[:].indirect(lst[:]))
             return picked
 
-        def gather_words(table, lst, name):
-            picked = pool.tile([P, J], U32, name=name + "_words", align_bytes=64)
-            nc.vector.tensor_copy(picked[:], table[:].indirect(lst[:]))
-            return picked
+        w_codes = pool.tile([P, 2, PACK, P], U16, name="w_codes", align_bytes=64)
+        for i in range(2):
+            nc.scalar.copy(w_codes[:, i], w_raw[:, i].rearrange("p (m t) -> p t m", t=PACK))
 
-        w_codes = pool.tile([P, PACK, 2, P], U16, name="w_codes", align_bytes=64)
-        w_planes = pool.tile([P, PACK, 2, P], U8, name="w_planes", align_bytes=64)
-        dealt_words = w_raw[:].rearrange("p i (m t) -> p t i m", t=PACK)
-        dealt_scales = ws_raw[:, 0, :].rearrange("p (i m t) -> p t i m", i=2, t=PACK)
-
-        def deal(t):
-            nc.vector.tensor_copy(w_codes[:, t], dealt_words[:, t])
-            nc.vector.tensor_copy(w_planes[:, t], dealt_scales[:, t])
-
-        xt_s = gather_scales(xt_stage, idx, "xt")
-        xo_s = gather_scales(xo_stage, idx2, "xo")
-        xt_w = gather_words(xt_table, idx, "xt")
+        xt_plane = spread_scales(xt_stage, "xt")
+        xo_plane = spread_scales(xo_stage, "xo")
+        xt_s = gather(xt_plane, idx, U8, "xt_s")
+        xo_s = gather(xo_plane, idx2, U8, "xo_s")
         nc.vector.tensor_copy(ws_raw[64:128, 0, :].bitcast(I32), ws_raw[0:64, 1, :].bitcast(I32))
-        deal(0)
-        xo_w = gather_words(xo_table, idx2, "xo")
+        xt_w = gather(xt_table, idx, U32, "xt_w")
+        dealt_scales = ws_raw[:, 0, :].rearrange("p (i m t) -> p t i m", i=2, t=PACK)
+        planes_first = pool.tile([P, 1, 2, P], U8, name="planes_first", align_bytes=64)
+        nc.vector.tensor_copy(planes_first[:], dealt_scales[:, 0:1])
+        xo_w = gather(xo_table, idx2, U32, "xo_w")
+        planes_rest = pool.tile([P, PACK - 1, 2, P], U8, name="planes_rest", tag="table_planes_page", align_bytes=64)
         hidden = []
         for t in range(PACK):
+            planes = planes_first[:, 0] if t == 0 else planes_rest[:, t - 1]
             acc = psum.tile([P, J], F32, name=f"acc{t}")
-            nc.tensor.matmul_mx(acc[:], lhsT=w_codes[:, t, 0].bitcast(E2M1), lhsT_scale=w_planes[:, t, 0],
+            nc.tensor.matmul_mx(acc[:], lhsT=w_codes[:, 0, t].bitcast(E2M1), lhsT_scale=planes[:, 0],
                                 rhs=xt_w[:].bitcast(E5M2), rhs_scale=xt_s[:], start=True, stop=False)
-            nc.tensor.matmul_mx(acc[:], lhsT=w_codes[:, t, 1].bitcast(E2M1), lhsT_scale=w_planes[:, t, 1],
+            nc.tensor.matmul_mx(acc[:], lhsT=w_codes[:, 1, t].bitcast(E2M1), lhsT_scale=planes[:, 1],
                                 rhs=xo_w[:].bitcast(E4M3), rhs_scale=xo_s[:], start=False, stop=True)
             if t + 1 < PACK:
-                deal(t + 1)
+                nc.vector.tensor_copy(planes_rest[:, t], dealt_scales[:, t + 1])
             rows = pool.tile([P, J], F32, name=f"hidden{t}")
             nc.vector.tensor_copy(rows[:], acc[:])
             hidden.append(rows)
 
+        pages = [
+            pool.tile([P, E], F32, name="page0", tag="scales_then_page"),
+            pool.tile([P, E], F32, name="page1", tag="table_planes_page", align_bytes=64),
+        ]
+        for page in pages:
+            nc.gpsimd.memset(page[:], 0.0)
+
         first = pool.tile([P, PACK, O], F32, name="first")
         second = pool.tile([P, PACK, O], F32, name="second")
-        gate = pool.tile([P, PACK, O], F32, name="gate")
+        gate_first = pool.tile([P, 1, O], F32, name="gate_first")
         diff = pool.tile([P, PACK, O], F32, name="diff")
         size = pool.tile([P, PACK, O], F32, name="size")
         hid = pool.tile([P, O, PACK], BF16, name="hid", align_bytes=64)
 
-        def fetch_gate(t):
-            nc.scalar.activation(gate[:, t], hidden[t][:].indirect(idx5[:]), ACT.Sigmoid,
+        def fetch_gate(dst, t):
+            nc.scalar.activation(dst, hidden[t][:].indirect(idx5[:]), ACT.Sigmoid,
                                  bias=cols["bg"][:, t : t + 1], scale=cols["sg"][:, t : t + 1])
 
         def fetch_pair(t):
@@ -142,27 +144,32 @@ def tile_list_gatedlarger_bank_one_scattered_kernel(
         def magnitude(ts):
             nc.vector.scalar_tensor_tensor(size[:, ts], diff[:, ts], -1.0, diff[:, ts], ALU.mult, ALU.max)
 
-        def gated(ts):
-            nc.vector.tensor_tensor(hid[:, :, ts], size[:, ts].rearrange("p t o -> p o t"),
-                                    gate[:, ts].rearrange("p t o -> p o t"), ALU.mult)
+        def gated(gate, ts, places):
+            nc.vector.tensor_tensor(hid[:, places, ts], size[:, ts, places].rearrange("p t o -> p o t"),
+                                    gate[:, :, places].rearrange("p t o -> p o t"), ALU.mult)
 
-        fetch_gate(0)
+        fetch_gate(gate_first[:, 0], 0)
         for t in range(PACK):
             fetch_pair(t)
+        gate_rest = pool.tile([P, PACK - 1, O], F32, name="gate_rest", tag="sa_cols")
         for t in range(1, PACK):
-            fetch_gate(t)
+            fetch_gate(gate_rest[:, t - 1], t)
         subtract(slice(0, 2))
         magnitude(slice(0, 2))
         subtract(slice(2, 3))
-        gated(slice(0, 1))
+        gated(gate_first, slice(0, 1), slice(0, O))
         magnitude(slice(2, 3))
         subtract(slice(3, 4))
         magnitude(slice(3, 4))
-        gated(slice(1, 4))
+        halves = (slice(0, O // 2), slice(O // 2, O))
+        for places in halves:
+            gated(gate_rest, slice(1, 4), places)
 
         hid_words = pool.tile([P, O], U32, name="hid_words", align_bytes=64)
         hid_scales = pool.tile([P, O], U8, name="hid_scales", align_bytes=64)
-        nc.vector.quantize_mx(hid_words[:].bitcast(E4M3), hid_scales[:], hid[:].rearrange("p o t -> p (o t)"))
+        for places in halves:
+            nc.vector.quantize_mx(hid_words[:, places].bitcast(E4M3), hid_scales[:, places],
+                                  hid[:, places].rearrange("p o t -> p (o t)"))
 
         for h in range(2):
             acc = psum.tile([P, O], F32, name=f"result{h}")

from contextlib import ExitStack

import concourse.mybir as mybir

K, T, J, R, O, N, E = 512, 1024, 256, 512, 128, 256, 1024
P = 128
PACK = 4
FLOPS = 2 * K * R * J * 2 + 2 * R * N * O

F32 = mybir.dt.float32
BF16 = mybir.dt.bfloat16
I32 = mybir.dt.int32
U32 = mybir.dt.uint32
U16 = mybir.dt.uint16
U8 = mybir.dt.uint8
E4M3 = mybir.dt.float8_e4m3fn_x4
E5M2 = mybir.dt.float8_e5m2_x4
E2M1 = mybir.dt.float4_e2m1fn_x4
ACT = mybir.ActivationFunctionType
ALU = mybir.AluOpType


def tile_list_gatedlarger_bank_one_scattered_kernel(
    tc, xt_words, xt_scales, xo_words, xo_scales, w_words, w_scales, w0_words, w0_scales,
    sa, sb, sg, bg, wb_words, wb_scales, offs, offs2, offs3, offs4, offs5, offs6, out,
):
    nc = tc.nc
    with ExitStack() as ctx:
        pool = ctx.enter_context(tc.tile_pool(name="held", bufs=1))
        psum = ctx.enter_context(tc.psum_pool(name="psum", bufs=1))

        def load_list(src, name):
            lst = pool.tile(list(src.shape), U16, name=name)
            nc.sync.dma_start(lst[:], src)
            return lst

        def half_rows(scales):
            return scales[0].bitcast(I32).rearrange("(h g r) n -> g r h n", h=2, g=2)

        def load_half_rows(queue, dst, scales):
            for g in range(2):
                queue.dma_start(dst[32 * g : 32 * g + 4].bitcast(I32), half_rows(scales)[g])

        xt_stage = pool.tile([64, 2, T], U8, name="xt_stage")
        xo_stage = pool.tile([64, 2, T], U8, name="xo_stage")
        ws_raw = pool.tile([P, 2, 2 * R], U8, name="ws_raw", tag="scales_then_page")
        wb_plane = pool.tile([P, N], U8, name="wb_plane", align_bytes=64)
        for stage in (xt_stage, xo_stage, ws_raw):
            nc.vector.memset(stage[0:64, 0].bitcast(I32), 0)
            nc.gpsimd.memset(stage[0:64, 1].bitcast(I32), 0)
        nc.vector.memset(wb_plane[:].bitcast(I32), 0)

        w_raw = pool.tile([P, 2, R], U16, name="w_raw")
        xt_table = pool.tile([P, T], U32, name="xt_table")
        xo_table = pool.tile([P, T], U32, name="xo_table", tag="table_planes_page", align_bytes=64)
        idx = load_list(offs, "idx")
        idx2 = load_list(offs2, "idx2")
        nc.sync.dma_start(w_raw[:, 0].bitcast(I32), w_words[0].bitcast(I32))
        load_half_rows(nc.sync, xt_stage, xt_scales)
        load_half_rows(nc.sync, xo_stage, xo_scales)
        nc.sync.dma_start(xt_table[:].bitcast(I32), xt_words[0].rearrange("p n t -> p (n t)").bitcast(I32))
        load_half_rows(nc.sync, ws_raw[:, :, 0:R], w_scales)
        load_half_rows(nc.sync, ws_raw[:, :, R : 2 * R], w0_scales)
        nc.sync.dma_start(w_raw[:, 1].bitcast(I32), w0_words[0].bitcast(I32))
        nc.sync.dma_start(xo_table[:].bitcast(I32), xo_words[0].rearrange("p n t -> p (n t)").bitcast(I32))
        idx5 = load_list(offs5, "idx5")
        idx3 = load_list(offs3, "idx3")
        idx4 = load_list(offs4, "idx4")
        cols = {}
        for name, src in (("sg", sg), ("bg", bg), ("sa", sa), ("sb", sb)):
            cols[name] = pool.tile([P, PACK], F32, name=name + "_cols", tag=name + "_cols")
            nc.gpsimd.dma_start(cols[name][:], src.rearrange("(p t) one -> p (t one)", t=PACK))
        idx6 = load_list(offs6, "idx6")
        wb_codes = pool.tile([P, 2 * N], U8, name="wb_codes", align_bytes=64)
        nc.sync.dma_start(wb_codes[:].bitcast(I32), wb_words[0].bitcast(I32))
        for q in range(4):
            nc.sync.dma_start(wb_plane[32 * q : 32 * q + 4, :].bitcast(I32), wb_scales[0, 4 * q : 4 * q + 4, :].bitcast(I32))

        def spread_scales(stage, name):
            plane = pool.tile([P, T], U8, name=name + "_plane")
            for h in range(2):
                nc.vector.tensor_copy(plane[64 * h : 64 * h + 64, :].bitcast(I32), stage[:, h, :].bitcast(I32))
            return plane

        def gather(window, lst, dtype, name):
            picked = pool.tile([P, J], dtype, name=name, align_bytes=64)
            nc.vector.tensor_copy(picked[:], window[:].indirect(lst[:]))
            return picked

        w_codes = pool.tile([P, 2, PACK, P], U16, name="w_codes", align_bytes=64)
        for i in range(2):
            nc.scalar.copy(w_codes[:, i], w_raw[:, i].rearrange("p (m t) -> p t m", t=PACK))

        xt_plane = spread_scales(xt_stage, "xt")
        xo_plane = spread_scales(xo_stage, "xo")
        xt_s = gather(xt_plane, idx, U8, "xt_s")
        xo_s = gather(xo_plane, idx2, U8, "xo_s")
        nc.vector.tensor_copy(ws_raw[64:128, 0, :].bitcast(I32), ws_raw[0:64, 1, :].bitcast(I32))
        xt_w = gather(xt_table, idx, U32, "xt_w")
        dealt_scales = ws_raw[:, 0, :].rearrange("p (i m t) -> p t i m", i=2, t=PACK)
        planes_first = pool.tile([P, 1, 2, P], U8, name="planes_first", align_bytes=64)
        nc.vector.tensor_copy(planes_first[:], dealt_scales[:, 0:1])
        xo_w = gather(xo_table, idx2, U32, "xo_w")
        planes_rest = pool.tile([P, PACK - 1, 2, P], U8, name="planes_rest", tag="table_planes_page", align_bytes=64)
        hidden = []
        for t in range(PACK):
            planes = planes_first[:, 0] if t == 0 else planes_rest[:, t - 1]
            acc = psum.tile([P, J], F32, name=f"acc{t}")
            nc.tensor.matmul_mx(acc[:], lhsT=w_codes[:, 0, t].bitcast(E2M1), lhsT_scale=planes[:, 0],
                                rhs=xt_w[:].bitcast(E5M2), rhs_scale=xt_s[:], start=True, stop=False)
            nc.tensor.matmul_mx(acc[:], lhsT=w_codes[:, 1, t].bitcast(E2M1), lhsT_scale=planes[:, 1],
                                rhs=xo_w[:].bitcast(E4M3), rhs_scale=xo_s[:], start=False, stop=True)
            if t + 1 < PACK:
                nc.vector.tensor_copy(planes_rest[:, t], dealt_scales[:, t + 1])
            rows = pool.tile([P, J], F32, name=f"hidden{t}")
            nc.vector.tensor_copy(rows[:], acc[:])
            hidden.append(rows)

        pages = [
            pool.tile([P, E], F32, name="page0", tag="scales_then_page"),
            pool.tile([P, E], F32, name="page1", tag="table_planes_page", align_bytes=64),
        ]
        for page in pages:
            nc.gpsimd.memset(page[:], 0.0)

        first = pool.tile([P, PACK, O], F32, name="first")
        second = pool.tile([P, PACK, O], F32, name="second")
        gate_first = pool.tile([P, 1, O], F32, name="gate_first")
        diff = pool.tile([P, PACK, O], F32, name="diff")
        size = pool.tile([P, PACK, O], F32, name="size")
        hid = pool.tile([P, O, PACK], BF16, name="hid", align_bytes=64)

        def fetch_gate(dst, t):
            nc.scalar.activation(dst, hidden[t][:].indirect(idx5[:]), ACT.Sigmoid,
                                 bias=cols["bg"][:, t : t + 1], scale=cols["sg"][:, t : t + 1])

        def fetch_pair(t):
            nc.scalar.activation(first[:, t], hidden[t][:].indirect(idx3[:]), ACT.Copy, scale=cols["sa"][:, t : t + 1])
            nc.scalar.activation(second[:, t], hidden[t][:].indirect(idx4[:]), ACT.Copy, scale=cols["sb"][:, t : t + 1])

        def subtract(ts):
            nc.vector.tensor_tensor(diff[:, ts], first[:, ts], second[:, ts], ALU.subtract)

        def magnitude(ts):
            nc.vector.scalar_tensor_tensor(size[:, ts], diff[:, ts], -1.0, diff[:, ts], ALU.mult, ALU.max)

        def gated(gate, ts, places):
            nc.vector.tensor_tensor(hid[:, places, ts], size[:, ts, places].rearrange("p t o -> p o t"),
                                    gate[:, :, places].rearrange("p t o -> p o t"), ALU.mult)

        fetch_gate(gate_first[:, 0], 0)
        for t in range(PACK):
            fetch_pair(t)
        gate_rest = pool.tile([P, PACK - 1, O], F32, name="gate_rest", tag="sa_cols")
        for t in range(1, PACK):
            fetch_gate(gate_rest[:, t - 1], t)
        subtract(slice(0, 2))
        magnitude(slice(0, 2))
        subtract(slice(2, 3))
        gated(gate_first, slice(0, 1), slice(0, O))
        magnitude(slice(2, 3))
        subtract(slice(3, 4))
        magnitude(slice(3, 4))
        halves = (slice(0, O // 2), slice(O // 2, O))
        for places in halves:
            gated(gate_rest, slice(1, 4), places)

        hid_words = pool.tile([P, O], U32, name="hid_words", align_bytes=64)
        hid_scales = pool.tile([P, O], U8, name="hid_scales", align_bytes=64)
        for places in halves:
            nc.vector.quantize_mx(hid_words[:, places].bitcast(E4M3), hid_scales[:, places],
                                  hid[:, places].rearrange("p o t -> p (o t)"))

        for h in range(2):
            acc = psum.tile([P, O], F32, name=f"result{h}")
            nc.tensor.matmul_mx(acc[:], lhsT=wb_codes[:, 2 * P * h : 2 * P * (h + 1)].bitcast(E2M1),
                                lhsT_scale=wb_plane[:, P * h : P * (h + 1)],
                                rhs=hid_words[:].bitcast(E4M3), rhs_scale=hid_scales[:], start=True, stop=True)
            values = pool.tile([P, O], F32, name=f"values{h}")
            if h == 0:
                nc.vector.tensor_copy(values[:], acc[:])
                nc.vector.tensor_copy(pages[h][:].indirect(idx6[:]), values[:])
                nc.sync.dma_start(out[P * h : P * (h + 1), :], pages[h][:])
            else:
                nc.scalar.copy(values[:], acc[:])
                nc.scalar.activation(pages[h][:].indirect(idx6[:]), values[:], ACT.Copy)
                nc.scalar.dma_start(out[P * h : P * (h + 1), :], pages[h][:])
